import numpy as np
import ml_dtypes

BF16 = ml_dtypes.bfloat16


def bf(x):
    return np.asarray(x, np.float32).astype(BF16)


def f32(x):
    return np.asarray(x, np.float32)


def f64(x):
    return np.asarray(x).astype(np.float64)


def striped(idx):
    return np.tile(idx.reshape(-1, 16).T, (8, 1))


def rows(idx, k):
    return np.tile(idx, (k, 1))


def look(tab, idx):
    return np.take_along_axis(f64(tab), rows(idx, len(tab)), axis=1)


K, S, V, N, M = 256, 2048, 1536, 1536, 128


def silu(v):
    return v / (1.0 + np.exp(-v))


def setup_inputs():
    return {"tab": bf(np.random.standard_normal((K, S))), "y": f32(np.random.standard_normal((K, V))), "w": bf(np.random.standard_normal((K, M)) / np.sqrt(K)), "b": f32(0.5 * np.random.standard_normal((M, 1))), "offs": striped(np.random.permutation(S)[:N])}


def reference(tab, y, w, b, offs):
    idx = offs[:16].T.reshape(-1)
    t = look(tab, idx)
    x = silu(t) * f64(y)
    y = f64(w).T @ x
    return np.maximum(y + f64(b), 0.0)

@@ -1,0 +1,48 @@
+import concourse.mybir as mybir
+
+P = 128
+K, S, N, M = 256, 2048, 1536, 128
+BLOCKS = K // P
+PIECE = 512
+GROUP = 16
+
+FLOPS = 2 * K * M * N
+
+BF16, F32, U16 = mybir.dt.bfloat16, mybir.dt.float32, mybir.dt.uint16
+ALU = mybir.AluOpType
+SILU = mybir.ActivationFunctionType.Silu
+
+
+def tile_lookup_gate_silu_relu_kernel(tc, tab, y, w, b, offs, out):
+    nc = tc.nc
+    y_blocks = y.rearrange("(k p) n -> p k n", p=P)
+    with (
+        tc.tile_pool(name="held", bufs=1) as held,
+        tc.psum_pool(name="psum", bufs=1) as psum,
+    ):
+        offsets = held.tile([P, N // GROUP], U16, name="offsets")
+        windows = [held.tile([P, S], BF16, name=f"window{k}") for k in range(BLOCKS)]
+        streams = [held.tile([P, BLOCKS, PIECE], F32, name=f"stream{i}") for i in range(N // PIECE)]
+        weights = held.tile([P, BLOCKS, M], BF16, name="weights")
+        bias = held.tile([M, 1], F32, name="bias")
+
+        nc.sync.dma_start(offsets[:], offs)
+        for k in range(BLOCKS):
+            nc.sync.dma_start(windows[k][:], tab[k * P : (k + 1) * P, :])
+        nc.sync.dma_start(weights[:], w.rearrange("(k p) m -> p k m", p=P))
+        nc.sync.dma_start(bias[:], b)
+        for i in range(N // PIECE):
+            nc.sync.dma_start(streams[i][:], y_blocks[:, :, i * PIECE : (i + 1) * PIECE])
+
+        for i in range(N // PIECE):
+            entries = offsets[:, i * PIECE // GROUP : (i + 1) * PIECE // GROUP]
+            product = psum.tile([M, PIECE], F32, name=f"product{i}")
+            for k in range(BLOCKS):
+                gate = held.tile([P, PIECE], F32, name=f"gate{i}_{k}")
+                x = held.tile([P, PIECE], BF16, name=f"x{i}_{k}")
+                nc.scalar.activation(gate[:], windows[k][:].indirect(entries), SILU)
+                nc.vector.tensor_tensor(x[:], gate[:], streams[i][:, k, :], ALU.mult)
+                nc.tensor.matmul(product[:], weights[:, k, :], x[:], start=(k == 0), stop=(k == BLOCKS - 1))
+            result = held.tile([M, PIECE], F32, name=f"result{i}")
+            nc.vector.tensor_scalar(result[:], product[:], bias[:], 0.0, ALU.add, ALU.max)
+            nc.sync.dma_start(out[:, i * PIECE : (i + 1) * PIECE], result[:])

@@ -26,6 +26,10 @@ def tile_lookup_gate_silu_relu_kernel(tc, tab, y, w, b, offs, out):
         weights = held.tile([P, BLOCKS, M], BF16, name="weights")
         bias = held.tile([M, 1], F32, name="bias")
 
+        warm = held.tile([P, 8], F32, name="warm")
+        nc.vector.memset(warm[:], 0.0)
+        nc.scalar.activation(warm[:], warm[:], SILU)
+
         nc.sync.dma_start(offsets[:], offs)
         for k in range(BLOCKS):
             nc.sync.dma_start(windows[k][:], tab[k * P : (k + 1) * P, :])

@@ -3,50 +3,74 @@ import concourse.mybir as mybir
 P = 128
 K, S, N, M = 256, 2048, 1536, 128
 BLOCKS = K // P
-PIECE = 512
 GROUP = 16
+CHUNK = 512
+PIECE = 256
+PIECES = N // PIECE
+AHEAD = 3
 
 FLOPS = 2 * K * M * N
 
 BF16, F32, U16 = mybir.dt.bfloat16, mybir.dt.float32, mybir.dt.uint16
 ALU = mybir.AluOpType
-SILU = mybir.ActivationFunctionType.Silu
+ACT = mybir.ActivationFunctionType
 
 
 def tile_lookup_gate_silu_relu_kernel(tc, tab, y, w, b, offs, out):
     nc = tc.nc
-    y_blocks = y.rearrange("(k p) n -> p k n", p=P)
     with (
         tc.tile_pool(name="held", bufs=1) as held,
+        tc.tile_pool(name="ring", bufs=AHEAD) as ring,
         tc.psum_pool(name="psum", bufs=1) as psum,
     ):
         offsets = held.tile([P, N // GROUP], U16, name="offsets")
         windows = [held.tile([P, S], BF16, name=f"window{k}") for k in range(BLOCKS)]
-        streams = [held.tile([P, BLOCKS, PIECE], F32, name=f"stream{i}") for i in range(N // PIECE)]
+        streams = [
+            [held.tile([P, CHUNK], F32, name=f"stream{c}_{k}") for k in range(BLOCKS)] for c in range(N // CHUNK)
+        ]
         weights = held.tile([P, BLOCKS, M], BF16, name="weights")
         bias = held.tile([M, 1], F32, name="bias")
 
         warm = held.tile([P, 8], F32, name="warm")
         nc.vector.memset(warm[:], 0.0)
-        nc.scalar.activation(warm[:], warm[:], SILU)
+        nc.scalar.activation(warm[:], warm[:], ACT.Silu)
 
+        def load_stream(c):
+            for k in range(BLOCKS):
+                nc.sync.dma_start(streams[c][k][:], y[k * P : (k + 1) * P, c * CHUNK : (c + 1) * CHUNK])
+
+        nc.sync.dma_start(windows[0][:], tab[0:P, :])
         nc.sync.dma_start(offsets[:], offs)
-        for k in range(BLOCKS):
-            nc.sync.dma_start(windows[k][:], tab[k * P : (k + 1) * P, :])
+        nc.sync.dma_start(windows[1][:], tab[P : 2 * P, :])
+        load_stream(0)
         nc.sync.dma_start(weights[:], w.rearrange("(k p) m -> p k m", p=P))
         nc.sync.dma_start(bias[:], b)
-        for i in range(N // PIECE):
-            nc.sync.dma_start(streams[i][:], y_blocks[:, :, i * PIECE : (i + 1) * PIECE])
+        for c in range(1, N // CHUNK):
+            load_stream(c)
 
-        for i in range(N // PIECE):
-            entries = offsets[:, i * PIECE // GROUP : (i + 1) * PIECE // GROUP]
-            product = psum.tile([M, PIECE], F32, name=f"product{i}")
-            for k in range(BLOCKS):
-                gate = held.tile([P, PIECE], F32, name=f"gate{i}_{k}")
-                x = held.tile([P, PIECE], BF16, name=f"x{i}_{k}")
-                nc.scalar.activation(gate[:], windows[k][:].indirect(entries), SILU)
-                nc.vector.tensor_tensor(x[:], gate[:], streams[i][:, k, :], ALU.mult)
-                nc.tensor.matmul(product[:], weights[:, k, :], x[:], start=(k == 0), stop=(k == BLOCKS - 1))
+        products = [psum.tile([M, PIECE], F32, name=f"product{i}") for i in range(PIECES)]
+
+        def contract(i, k, gates):
+            start = i * PIECE
+            entries = offsets[:, start // GROUP : (start + PIECE) // GROUP]
+            stream = streams[start // CHUNK][k][:, start % CHUNK : start % CHUNK + PIECE]
+            x = held.tile([P, PIECE], BF16, name=f"x{i}_{k}")
+            nc.scalar.activation(gates[:, k, :], windows[k][:].indirect(entries), ACT.Silu)
+            nc.vector.tensor_tensor(x[:], gates[:, k, :], stream, ALU.mult)
+            nc.tensor.matmul(products[i][:], weights[:, k, :], x[:], start=(k == 0), stop=(k == BLOCKS - 1))
+
+        def finish(i):
             result = held.tile([M, PIECE], F32, name=f"result{i}")
-            nc.vector.tensor_scalar(result[:], product[:], bias[:], 0.0, ALU.add, ALU.max)
+            if i == PIECES - 1:
+                nc.scalar.activation(result[:], products[i][:], ACT.Relu, bias=bias[:])
+            else:
+                nc.vector.tensor_scalar(result[:], products[i][:], bias[:], 0.0, ALU.add, ALU.max)
             nc.sync.dma_start(out[:, i * PIECE : (i + 1) * PIECE], result[:])
+
+        for i in range(PIECES):
+            gates = ring.tile([P, BLOCKS, PIECE], F32, name="gates")
+            contract(i, 0, gates)
+            if i > 0:
+                finish(i - 1)
+            contract(i, 1, gates)
+        finish(PIECES - 1)

@@ -6,7 +6,8 @@ BLOCKS = K // P
 GROUP = 16
 CHUNK = 512
 PIECE = 256
-PIECES = N // PIECE
+PIECES = [(start, PIECE) for start in range(0, N - PIECE, PIECE)]
+PIECES = PIECES + [(N - PIECE, PIECE // 2), (N - PIECE // 2, PIECE // 2)]
 AHEAD = 3
 
 FLOPS = 2 * K * M * N
@@ -48,29 +49,30 @@ def tile_lookup_gate_silu_relu_kernel(tc, tab, y, w, b, offs, out):
         for c in range(1, N // CHUNK):
             load_stream(c)
 
-        products = [psum.tile([M, PIECE], F32, name=f"product{i}") for i in range(PIECES)]
+        products = [psum.tile([M, width], F32, name=f"product{i}") for i, (start, width) in enumerate(PIECES)]
 
         def contract(i, k, gates):
-            start = i * PIECE
-            entries = offsets[:, start // GROUP : (start + PIECE) // GROUP]
-            stream = streams[start // CHUNK][k][:, start % CHUNK : start % CHUNK + PIECE]
-            x = held.tile([P, PIECE], BF16, name=f"x{i}_{k}")
+            start, width = PIECES[i]
+            entries = offsets[:, start // GROUP : (start + width) // GROUP]
+            stream = streams[start // CHUNK][k][:, start % CHUNK : start % CHUNK + width]
+            x = held.tile([P, width], BF16, name=f"x{i}_{k}")
             nc.scalar.activation(gates[:, k, :], windows[k][:].indirect(entries), ACT.Silu)
             nc.vector.tensor_tensor(x[:], gates[:, k, :], stream, ALU.mult)
             nc.tensor.matmul(products[i][:], weights[:, k, :], x[:], start=(k == 0), stop=(k == BLOCKS - 1))
 
         def finish(i):
-            result = held.tile([M, PIECE], F32, name=f"result{i}")
-            if i == PIECES - 1:
+            start, width = PIECES[i]
+            result = held.tile([M, width], F32, name=f"result{i}")
+            if i == len(PIECES) - 1:
                 nc.scalar.activation(result[:], products[i][:], ACT.Relu, bias=bias[:])
             else:
                 nc.vector.tensor_scalar(result[:], products[i][:], bias[:], 0.0, ALU.add, ALU.max)
-            nc.sync.dma_start(out[:, i * PIECE : (i + 1) * PIECE], result[:])
+            nc.sync.dma_start(out[:, start : start + width], result[:])
 
-        for i in range(PIECES):
-            gates = ring.tile([P, BLOCKS, PIECE], F32, name="gates")
+        for i, (start, width) in enumerate(PIECES):
+            gates = ring.tile([P, BLOCKS, width], F32, name="gates")
             contract(i, 0, gates)
             if i > 0:
                 finish(i - 1)
             contract(i, 1, gates)
-        finish(PIECES - 1)
+        finish(len(PIECES) - 1)

import concourse.mybir as mybir

P = 128
K, S, N, M = 256, 2048, 1536, 128
BLOCKS = K // P
GROUP = 16
CHUNK = 512
PIECE = 256
PIECES = [(start, PIECE) for start in range(0, N - PIECE, PIECE)]
PIECES = PIECES + [(N - PIECE, PIECE // 2), (N - PIECE // 2, PIECE // 2)]
AHEAD = 3

FLOPS = 2 * K * M * N

BF16, F32, U16 = mybir.dt.bfloat16, mybir.dt.float32, mybir.dt.uint16
ALU = mybir.AluOpType
ACT = mybir.ActivationFunctionType


def tile_lookup_gate_silu_relu_kernel(tc, tab, y, w, b, offs, out):
    nc = tc.nc
    with (
        tc.tile_pool(name="held", bufs=1) as held,
        tc.tile_pool(name="ring", bufs=AHEAD) as ring,
        tc.psum_pool(name="psum", bufs=1) as psum,
    ):
        offsets = held.tile([P, N // GROUP], U16, name="offsets")
        windows = [held.tile([P, S], BF16, name=f"window{k}") for k in range(BLOCKS)]
        streams = [
            [held.tile([P, CHUNK], F32, name=f"stream{c}_{k}") for k in range(BLOCKS)] for c in range(N // CHUNK)
        ]
        weights = held.tile([P, BLOCKS, M], BF16, name="weights")
        bias = held.tile([M, 1], F32, name="bias")

        warm = held.tile([P, 8], F32, name="warm")
        nc.vector.memset(warm[:], 0.0)
        nc.scalar.activation(warm[:], warm[:], ACT.Silu)

        def load_stream(c):
            for k in range(BLOCKS):
                nc.sync.dma_start(streams[c][k][:], y[k * P : (k + 1) * P, c * CHUNK : (c + 1) * CHUNK])

        nc.sync.dma_start(windows[0][:], tab[0:P, :])
        nc.sync.dma_start(offsets[:], offs)
        nc.sync.dma_start(windows[1][:], tab[P : 2 * P, :])
        load_stream(0)
        nc.sync.dma_start(weights[:], w.rearrange("(k p) m -> p k m", p=P))
        nc.sync.dma_start(bias[:], b)
        for c in range(1, N // CHUNK):
            load_stream(c)

        products = [psum.tile([M, width], F32, name=f"product{i}") for i, (start, width) in enumerate(PIECES)]

        def contract(i, k, gates):
            start, width = PIECES[i]
            entries = offsets[:, start // GROUP : (start + width) // GROUP]
            stream = streams[start // CHUNK][k][:, start % CHUNK : start % CHUNK + width]
            x = held.tile([P, width], BF16, name=f"x{i}_{k}")
            nc.scalar.activation(gates[:, k, :], windows[k][:].indirect(entries), ACT.Silu)
            nc.vector.tensor_tensor(x[:], gates[:, k, :], stream, ALU.mult)
            nc.tensor.matmul(products[i][:], weights[:, k, :], x[:], start=(k == 0), stop=(k == BLOCKS - 1))

        def finish(i):
            start, width = PIECES[i]
            result = held.tile([M, width], F32, name=f"result{i}")
            if i == len(PIECES) - 1:
                nc.scalar.activation(result[:], products[i][:], ACT.Relu, bias=bias[:])
            else:
                nc.vector.tensor_scalar(result[:], products[i][:], bias[:], 0.0, ALU.add, ALU.max)
            nc.sync.dma_start(out[:, start : start + width], result[:])

        for i, (start, width) in enumerate(PIECES):
            gates = ring.tile([P, BLOCKS, width], F32, name="gates")
            contract(i, 0, gates)
            if i > 0:
                finish(i - 1)
            contract(i, 1, gates)
        finish(len(PIECES) - 1)
